import numpy as np
import ml_dtypes


def mxq(x, axis, fmt="e4m3"):
    dtype, down = {"e4m3": (ml_dtypes.float8_e4m3fn, 7), "e5m2": (ml_dtypes.float8_e5m2, 14)}[fmt]
    v = np.moveaxis(np.asarray(x, np.float32).astype(ml_dtypes.bfloat16).astype(np.float64), axis, -1)
    blocks = v.reshape(v.shape[:-1] + (-1, 32))
    amax = np.abs(blocks).max(-1, keepdims=True)
    byte = np.maximum(np.where(amax > 0, np.frexp(amax)[1] - 1 + 127, 0) - down, 1)
    scale = np.exp2(byte - 127.0)
    codes = (blocks / scale).astype(np.float32).astype(dtype).astype(np.float64)
    return np.moveaxis((codes * scale).reshape(v.shape), -1, axis)


WIDE = False


def mx_kscale(k):
    if not WIDE:
        return np.ones(k)
    levels = np.array([30, -30])
    if k % 512:
        return np.exp2(np.random.permutation(np.resize(levels, k // 32))).repeat(32)
    a = np.empty((k // 512, 16))
    for p in range(k // 512):
        a[p, :8] = np.random.permutation(np.resize(levels, 8))
        for g in range(8):
            far = levels[np.abs(levels - a[p, g]) >= 10]
            a[p, g + 8] = far[np.random.randint(len(far))]
    return np.exp2(a.ravel()).repeat(32)


def f64(x):
    return np.asarray(x).astype(np.float64)


def striped(idx):
    return np.tile(np.asarray(idx).reshape(-1, 16).T, (8, 1)).astype(np.uint16)


def unstriped(offs):
    return offs[:16].T.reshape(-1).astype(np.int64)


E2M1 = np.array([0.0, 0.5, 1.0, 1.5, 2.0, 3.0, 4.0, 6.0, -0.0, -0.5, -1.0, -1.5, -2.0, -3.0, -4.0, -6.0])


def pack_weight(w, fmt):
    k, n = w.shape
    w = f64(np.asarray(w, np.float32).astype(ml_dtypes.bfloat16)).reshape(k // 32, 32, n)
    amax = np.abs(w).max(1)
    if fmt in ("e4m3", "e5m2"):
        byte = np.frexp(amax)[1] - 1 + 127 - (7 if fmt == "e4m3" else 14)
    else:
        mant, ex = np.frexp(amax / 6.0)
        byte = np.where(mant > 0.5, ex, ex - 1) + 127
    byte = np.clip(np.where(amax > 0, byte, 1), 1, 254)
    scaled = (w * np.exp2(127.0 - byte)[:, None, :]).reshape(k, n).astype(np.float32)
    by_word = np.ascontiguousarray(scaled.reshape(k // 512, 128, 4, n).transpose(0, 1, 3, 2))
    if fmt in ("e4m3", "e5m2"):
        words = by_word.astype(ml_dtypes.float8_e4m3fn if fmt == "e4m3" else ml_dtypes.float8_e5m2).view(np.uint8)
    else:
        c = by_word.astype(ml_dtypes.float4_e2m1fn).view(np.uint8) & 0xF
        words = (c[..., 0::2] | (c[..., 1::2] << 4)).reshape(k // 512, 128, 2 * n)
    return np.ascontiguousarray(words), np.ascontiguousarray(byte.astype(np.uint8).reshape(k // 512, 16, n))


def unpack_weight(words, scales, fmt):
    g, _, n = scales.shape
    words = np.ascontiguousarray(words).reshape(g, 128, n, -1)
    if fmt in ("e4m3", "e5m2"):
        vals = words.view(ml_dtypes.float8_e4m3fn if fmt == "e4m3" else ml_dtypes.float8_e5m2).astype(np.float64)
    else:
        nib = np.empty((g, 128, n, 4), np.uint8)
        nib[..., 0::2] = words & 0xF
        nib[..., 1::2] = words >> 4
        vals = E2M1[nib]
    vals = vals * np.repeat(np.exp2(scales.astype(np.float64) - 127.0), 8, axis=1)[..., None]
    return vals.transpose(0, 1, 3, 2).reshape(g * 512, n)


K, T, J, R, O, N, L, E = 512, 2048, 256, 512, 128, 256, 512, 1024


def setup_inputs():
    n = np.random.standard_normal
    idx = np.random.permutation(T)[:J]
    idx2 = np.random.permutation(T)[:J]
    idx3 = np.random.permutation(J)[:O]
    idx4 = np.random.permutation(J)[:O]
    idx5 = np.random.permutation(E)[:O]
    fk = mx_kscale(K)
    fr = mx_kscale(R)
    fl = mx_kscale(L)
    xtp = pack_weight(n((K, T)) / fk[:, None], "e5m2")
    wp = pack_weight(n((K, R)) * 1 / np.sqrt(K) * fk[:, None] * fr, "e2m1")
    wbp = pack_weight(n((R, N)) * 1 / np.sqrt(R) / fr[:, None], "e2m1")
    sxp = pack_weight(n((L, O)) / fl[:, None], "e4m3")
    wsp = pack_weight(n((L, N)) * 1 / np.sqrt(L) * fl[:, None], "e2m1")
    return {
        "xt_words": xtp[0],
        "xt_scales": xtp[1],
        "w_words": wp[0],
        "w_scales": wp[1],
        "wb_words": wbp[0],
        "wb_scales": wbp[1],
        "sx_words": sxp[0],
        "sx_scales": sxp[1],
        "ws_words": wsp[0],
        "ws_scales": wsp[1],
        "tz": (n((N, E))).astype(np.float32),
        "offs": striped(idx),
        "offs2": striped(idx2),
        "offs3": striped(idx3),
        "offs4": striped(idx4),
        "offs5": striped(idx5),
    }


def reference(xt_words, xt_scales, w_words, w_scales, wb_words, wb_scales, sx_words, sx_scales, ws_words, ws_scales, tz, offs, offs2, offs3, offs4, offs5):
    idx = unstriped(offs)
    idx2 = unstriped(offs2)
    idx3 = unstriped(offs3)
    idx4 = unstriped(offs4)
    idx5 = unstriped(offs5)
    xtu = unpack_weight(xt_words, xt_scales, "e5m2")
    wu = unpack_weight(w_words, w_scales, "e2m1")
    wbu = unpack_weight(wb_words, wb_scales, "e2m1")
    sxu = unpack_weight(sx_words, sx_scales, "e4m3")
    wsu = unpack_weight(ws_words, ws_scales, "e2m1")
    xtidxg = xtu[:, idx]
    a = wu.T @ xtidxg
    xtidx2g = xtu[:, idx2]
    b = wu.T @ xtidx2g
    hid = np.abs(a[:, idx3] - b[:, idx4])
    hidq = mxq(hid, 0, "e4m3")
    p = wbu.T @ hidq + wsu.T @ sxu
    y = p + f64(tz)[:, idx5]
    return y

@@ -1,0 +1,186 @@
+from contextlib import ExitStack
+
+import concourse.mybir as mybir
+
+FLOPS = 335544320
+
+F32 = mybir.dt.float32
+BF16 = mybir.dt.bfloat16
+I32 = mybir.dt.int32
+U32 = mybir.dt.uint32
+U16 = mybir.dt.uint16
+U8 = mybir.dt.uint8
+E4M3X4 = mybir.dt.float8_e4m3fn_x4
+E5M2X4 = mybir.dt.float8_e5m2_x4
+E2M1X4 = mybir.dt.float4_e2m1fn_x4
+ACT = mybir.ActivationFunctionType
+ALU = mybir.AluOpType
+
+P = 128
+PACK = 4
+T, J, R, O, N, E = 2048, 256, 512, 128, 256, 1024
+
+
+def load_scale_rows(queues, plane, scales):
+    rows = scales[0].rearrange("(q r) c -> r q c", r=PACK)
+    for r in range(PACK):
+        queues[r].dma_start(out=plane[r:P:32, :].bitcast(I32), in_=rows[r].bitcast(I32))
+
+
+def tile_list_tied_looked_skip_tabled_kernel(
+    tc, xt_words, xt_scales, w_words, w_scales, wb_words, wb_scales, sx_words, sx_scales,
+    ws_words, ws_scales, tz, offs, offs2, offs3, offs4, offs5, out,
+):
+    nc = tc.nc
+    with ExitStack() as ctx:
+        lists = ctx.enter_context(tc.tile_pool(name="lists", bufs=1))
+        sb = ctx.enter_context(tc.tile_pool(name="sb", bufs=1))
+        psum = ctx.enter_context(tc.psum_pool(name="psum", bufs=1))
+
+        o1 = lists.tile([P, J // 16], U16, name="o1")
+        o2 = lists.tile([P, J // 16], U16, name="o2")
+        o3 = lists.tile([P, O // 16], U16, name="o3")
+        o4 = lists.tile([P, O // 16], U16, name="o4")
+        o5 = lists.tile([P, O // 16], U16, name="o5")
+
+        xw = sb.tile([P, T], U32, name="xw", align_bytes=64)
+        xs = sb.tile([P, T], U8, name="xs", align_bytes=64)
+        w_raw = sb.tile([P, R], U16, name="w_raw", align_bytes=64)
+        wsc_raw = sb.tile([P, R], U8, name="wsc_raw", tag="wsc_then_b", align_bytes=64)
+        w_dealt = sb.tile([P, PACK, P], U16, name="w_dealt", align_bytes=64)
+        wsc_dealt = sb.tile([P, PACK, P], U8, name="wsc_dealt", align_bytes=64)
+        late = sb.tile([P, 2 * N + O], U8, name="late", align_bytes=64)
+        wb_sc = late[:, 0:N]
+        ws_sc = late[:, N : 2 * N]
+        sx_sc = late[:, 2 * N : 2 * N + O]
+        wb_w = sb.tile([P, 2 * N], U8, name="wb_w", align_bytes=64)
+        ws_w = sb.tile([P, 2 * N], U8, name="ws_w", align_bytes=64)
+        sx_w = sb.tile([P, O], U32, name="sx_w", align_bytes=64)
+        tzt = sb.tile([P, 2, E], F32, name="tzt", align_bytes=64)
+
+        nc.vector.memset(xs[:].bitcast(I32), 0)
+        nc.vector.memset(wsc_raw[:].bitcast(I32), 0)
+        nc.vector.memset(late[:].bitcast(I32), 0)
+
+        xw_src = xt_words[0].rearrange("p c t -> p (c t)").bitcast(I32)
+        sx_src = sx_words[0].rearrange("p c t -> p (c t)").bitcast(I32)
+        S, A, G = nc.sync, nc.scalar, nc.gpsimd
+        S.dma_start(o1[:], offs)
+        A.dma_start(out=w_raw[:].bitcast(I32), in_=w_words[0].bitcast(I32))
+        S.dma_start(o2[:], offs2)
+        S.dma_start(out=xw[:, 0:2048].bitcast(I32), in_=xw_src[:, 0:2048])
+        load_scale_rows((A, A, A, A), xs, xt_scales)
+        load_scale_rows((S, S, S, G), wsc_raw, w_scales)
+        S.dma_start(o3[:], offs3)
+        S.dma_start(o4[:], offs4)
+        load_scale_rows((G, G, G, G), sx_sc, sx_scales)
+        load_scale_rows((S, S, S, S), ws_sc, ws_scales)
+        S.dma_start(out=ws_w[:].bitcast(I32), in_=ws_words[0].bitcast(I32))
+        S.dma_start(out=tzt[:], in_=tz.rearrange("(h p) e -> p h e", p=P))
+        S.dma_start(out=sx_w[:].bitcast(I32), in_=sx_src)
+        load_scale_rows((S, S, S, S), wb_sc, wb_scales)
+        S.dma_start(out=wb_w[:].bitcast(I32), in_=wb_words[0].bitcast(I32))
+        S.dma_start(o5[:], offs5)
+
+        ga_w = sb.tile([P, J], U32, name="ga_w", align_bytes=64)
+        ga_s = sb.tile([P, J], U8, name="ga_s", align_bytes=64)
+        gb_s = sb.tile([P, J], U8, name="gb_s", align_bytes=64)
+
+        nc.scalar.copy(out=w_dealt[:], in_=w_raw[:].rearrange("p (q t) -> p t q", t=PACK))
+        nc.vector.tensor_copy(out=ga_s[:], in_=xs[:].indirect(o1[:]))
+        nc.vector.tensor_copy(out=gb_s[:], in_=xs[:].indirect(o2[:]))
+        nc.vector.tensor_copy(out=ga_w[:], in_=xw[:].indirect(o1[:]))
+        nc.vector.tensor_copy(out=wsc_dealt[:], in_=wsc_raw[:].rearrange("p (q t) -> p t q", t=PACK))
+        gb_w = sb.tile([P, J], U32, name="gb_w", tag="wsc_then_b", align_bytes=64)
+        nc.vector.tensor_copy(out=gb_w[:], in_=xw[:].indirect(o2[:]))
+
+        banks = {}
+        whole = {}
+        picked = sb.tile([P, PACK, O], F32, name="picked", align_bytes=64)
+        diff = sb.tile([P, PACK, O], F32, name="diff", tag="diff", align_bytes=64)
+
+        def mm(side, t):
+            words, scales = (ga_w, ga_s) if side == "a" else (gb_w, gb_s)
+            bank = psum.tile([P, J], F32, name="bank_%s%d" % (side, t), tag="bank_%s%d" % (side, t))
+            banks[side, t] = bank
+            nc.tensor.matmul_mx(
+                out=bank[:], lhsT=w_dealt[:, t, :].bitcast(E2M1X4), lhsT_scale=wsc_dealt[:, t, :],
+                rhs=words[:].bitcast(E5M2X4), rhs_scale=scales[:], start=True, stop=True,
+            )
+
+        def cp(side, t, eng):
+            tile = sb.tile([P, J], F32, name="whole_%s%d" % (side, t), align_bytes=64)
+            whole[side, t] = tile
+            if eng == "S":
+                nc.scalar.activation(out=tile[:], in_=banks[side, t][:], func=ACT.Copy)
+            else:
+                nc.vector.tensor_copy(out=tile[:], in_=banks[side, t][:])
+
+        def ga(t, eng):
+            if eng == "S":
+                nc.scalar.activation(out=picked[:, t, :], in_=whole["a", t][:].indirect(o3[:]), func=ACT.Copy)
+            else:
+                nc.vector.tensor_copy(out=picked[:, t, :], in_=whole["a", t][:].indirect(o3[:]))
+
+        def gs(t):
+            nc.vector.tensor_tensor(
+                out=diff[:, t, :], in0=whole["b", t][:].indirect(o4[:]), in1=picked[:, t, :], op=ALU.subtract
+            )
+
+        mm("a", 0)
+        mm("a", 1)
+        mm("b", 0)
+        mm("b", 1)
+        mm("a", 2)
+        mm("b", 2)
+        mm("a", 3)
+        mm("b", 3)
+        cp("a", 0, "S")
+        cp("a", 1, "V")
+        ga(0, "S")
+        cp("b", 0, "V")
+        ga(1, "S")
+        gs(0)
+        cp("b", 1, "S")
+        cp("a", 2, "S")
+        gs(1)
+        ga(2, "S")
+        cp("b", 2, "V")
+        cp("a", 3, "S")
+        gs(2)
+        ga(3, "S")
+        cp("b", 3, "V")
+        gs(3)
+
+        acc = [psum.tile([P, O], F32, name="acc%d" % h, tag="bank_a%d" % h) for h in range(2)]
+        for h in range(2):
+            nc.tensor.matmul_mx(
+                out=acc[h][:], lhsT=ws_w[:, 2 * P * h : 2 * P * (h + 1)].bitcast(E2M1X4),
+                lhsT_scale=ws_sc[:, P * h : P * (h + 1)],
+                rhs=sx_w[:].bitcast(E4M3X4), rhs_scale=sx_sc, start=True, stop=False,
+            )
+
+        hid = sb.tile([P, O, PACK], BF16, name="hid", align_bytes=64)
+        nc.scalar.activation(
+            out=hid[:].rearrange("p (c i) t -> p c t i", i=4),
+            in_=diff[:].rearrange("p t (c i) -> p c t i", i=4),
+            func=ACT.Abs,
+        )
+        hq = sb.tile([P, O], U32, name="hq", align_bytes=64)
+        hs = sb.tile([P, O], U8, name="hs", align_bytes=64)
+        nc.vector.quantize_mx(out=hq[:].bitcast(E4M3X4), scales=hs[:], in_=hid[:].rearrange("p o t -> p (o t)"))
+
+        tzg = sb.tile([P, 2, O], F32, name="tzg", tag="diff", align_bytes=64)
+        for h in range(2):
+            nc.scalar.activation(out=tzg[:, h, :], in_=tzt[:, h, :].indirect(o5[:]), func=ACT.Copy)
+
+        for h in range(2):
+            nc.tensor.matmul_mx(
+                out=acc[h][:], lhsT=wb_w[:, 2 * P * h : 2 * P * (h + 1)].bitcast(E2M1X4),
+                lhsT_scale=wb_sc[:, P * h : P * (h + 1)],
+                rhs=hq[:].bitcast(E4M3X4), rhs_scale=hs[:], start=False, stop=True,
+            )
+        for h in range(2):
+            res = sb.tile([P, O], F32, name="res%d" % h, align_bytes=64)
+            nc.vector.tensor_tensor(out=res[:], in0=acc[h][:], in1=tzg[:, h, :], op=ALU.add)
+            (S, A)[h].dma_start(out=out[P * h : P * (h + 1), :], in_=res[:])

@@ -58,7 +58,8 @@ def tile_list_tied_looked_skip_tabled_kernel(
         sx_w = sb.tile([P, O], U32, name="sx_w", align_bytes=64)
         tzt = sb.tile([P, 2, E], F32, name="tzt", align_bytes=64)
 
-        nc.vector.memset(xs[:].bitcast(I32), 0)
+        nc.vector.memset(xs[:, 0 : T // 2].bitcast(I32), 0)
+        nc.gpsimd.memset(xs[:, T // 2 : T].bitcast(I32), 0)
         nc.vector.memset(wsc_raw[:].bitcast(I32), 0)
         nc.vector.memset(late[:].bitcast(I32), 0)
 
@@ -66,21 +67,21 @@ def tile_list_tied_looked_skip_tabled_kernel(
         sx_src = sx_words[0].rearrange("p c t -> p (c t)").bitcast(I32)
         S, A, G = nc.sync, nc.scalar, nc.gpsimd
         S.dma_start(o1[:], offs)
-        A.dma_start(out=w_raw[:].bitcast(I32), in_=w_words[0].bitcast(I32))
         S.dma_start(o2[:], offs2)
+        S.dma_start(out=w_raw[:].bitcast(I32), in_=w_words[0].bitcast(I32))
+        load_scale_rows((S, A, S, A), xs, xt_scales)
         S.dma_start(out=xw[:, 0:2048].bitcast(I32), in_=xw_src[:, 0:2048])
-        load_scale_rows((A, A, A, A), xs, xt_scales)
-        load_scale_rows((S, S, S, G), wsc_raw, w_scales)
+        load_scale_rows((S, S, S, S), wsc_raw, w_scales)
         S.dma_start(o3[:], offs3)
         S.dma_start(o4[:], offs4)
-        load_scale_rows((G, G, G, G), sx_sc, sx_scales)
+        load_scale_rows((G, G, G, S), sx_sc, sx_scales)
         load_scale_rows((S, S, S, S), ws_sc, ws_scales)
         S.dma_start(out=ws_w[:].bitcast(I32), in_=ws_words[0].bitcast(I32))
-        S.dma_start(out=tzt[:], in_=tz.rearrange("(h p) e -> p h e", p=P))
         S.dma_start(out=sx_w[:].bitcast(I32), in_=sx_src)
+        S.dma_start(out=tzt[:], in_=tz.rearrange("(h p) e -> p h e", p=P))
+        S.dma_start(o5[:], offs5)
         load_scale_rows((S, S, S, S), wb_sc, wb_scales)
         S.dma_start(out=wb_w[:].bitcast(I32), in_=wb_words[0].bitcast(I32))
-        S.dma_start(o5[:], offs5)
 
         ga_w = sb.tile([P, J], U32, name="ga_w", align_bytes=64)
         ga_s = sb.tile([P, J], U8, name="ga_s", align_bytes=64)
@@ -94,9 +95,10 @@ def tile_list_tied_looked_skip_tabled_kernel(
         gb_w = sb.tile([P, J], U32, name="gb_w", tag="wsc_then_b", align_bytes=64)
         nc.vector.tensor_copy(out=gb_w[:], in_=xw[:].indirect(o2[:]))
 
+        hid = sb.tile([P, O, PACK], BF16, name="hid", align_bytes=64)
         banks = {}
         whole = {}
-        picked = sb.tile([P, PACK, O], F32, name="picked", align_bytes=64)
+        picked = sb.tile([P, PACK, O], F32, name="picked", tag="picked", align_bytes=64)
         diff = sb.tile([P, PACK, O], F32, name="diff", tag="diff", align_bytes=64)
 
         def mm(side, t):
@@ -129,30 +131,32 @@ def tile_list_tied_looked_skip_tabled_kernel(
 
         mm("a", 0)
         mm("a", 1)
+        mm("a", 2)
         mm("b", 0)
         mm("b", 1)
-        mm("a", 2)
-        mm("b", 2)
         mm("a", 3)
+        mm("b", 2)
         mm("b", 3)
         cp("a", 0, "S")
         cp("a", 1, "V")
         ga(0, "S")
-        cp("b", 0, "V")
+        cp("a", 2, "V")
         ga(1, "S")
-        gs(0)
-        cp("b", 1, "S")
-        cp("a", 2, "S")
-        gs(1)
+        cp("b", 0, "V")
         ga(2, "S")
-        cp("b", 2, "V")
+        cp("b", 1, "V")
         cp("a", 3, "S")
-        gs(2)
+        gs(0)
+        cp("b", 2, "S")
+        gs(1)
+        cp("b", 3, "S")
         ga(3, "S")
-        cp("b", 3, "V")
+        gs(2)
+        nc.scalar.activation(out=hid[:, :, 0:2].rearrange("p (c i) t -> p c t i", i=4), in_=diff[:, 0:2, :].rearrange("p t (c i) -> p c t i", i=4), func=ACT.Abs)
         gs(3)
+        nc.scalar.activation(out=hid[:, :, 2:4].rearrange("p (c i) t -> p c t i", i=4), in_=diff[:, 2:4, :].rearrange("p t (c i) -> p c t i", i=4), func=ACT.Abs)
 
-        acc = [psum.tile([P, O], F32, name="acc%d" % h, tag="bank_a%d" % h) for h in range(2)]
+        acc = [psum.tile([P, O], F32, name="acc%d" % h, tag="bank_%s3" % "ab"[h]) for h in range(2)]
         for h in range(2):
             nc.tensor.matmul_mx(
                 out=acc[h][:], lhsT=ws_w[:, 2 * P * h : 2 * P * (h + 1)].bitcast(E2M1X4),
@@ -160,17 +164,12 @@ def tile_list_tied_looked_skip_tabled_kernel(
                 rhs=sx_w[:].bitcast(E4M3X4), rhs_scale=sx_sc, start=True, stop=False,
             )
 
-        hid = sb.tile([P, O, PACK], BF16, name="hid", align_bytes=64)
-        nc.scalar.activation(
-            out=hid[:].rearrange("p (c i) t -> p c t i", i=4),
-            in_=diff[:].rearrange("p t (c i) -> p c t i", i=4),
-            func=ACT.Abs,
-        )
+
         hq = sb.tile([P, O], U32, name="hq", align_bytes=64)
         hs = sb.tile([P, O], U8, name="hs", align_bytes=64)
         nc.vector.quantize_mx(out=hq[:].bitcast(E4M3X4), scales=hs[:], in_=hid[:].rearrange("p o t -> p (o t)"))
 
-        tzg = sb.tile([P, 2, O], F32, name="tzg", tag="diff", align_bytes=64)
+        tzg = sb.tile([P, 2, O], F32, name="tzg", tag="picked", align_bytes=64)
         for h in range(2):
             nc.scalar.activation(out=tzg[:, h, :], in_=tzt[:, h, :].indirect(o5[:]), func=ACT.Copy)
 

@@ -71,14 +71,14 @@ def tile_list_tied_looked_skip_tabled_kernel(
         S.dma_start(out=w_raw[:].bitcast(I32), in_=w_words[0].bitcast(I32))
         load_scale_rows((S, A, S, A), xs, xt_scales)
         S.dma_start(out=xw[:, 0:2048].bitcast(I32), in_=xw_src[:, 0:2048])
-        load_scale_rows((S, S, S, S), wsc_raw, w_scales)
+        load_scale_rows((S, S, S, G), wsc_raw, w_scales)
         S.dma_start(o3[:], offs3)
         S.dma_start(o4[:], offs4)
-        load_scale_rows((G, G, G, S), sx_sc, sx_scales)
+        load_scale_rows((G, G, S, S), sx_sc, sx_scales)
         load_scale_rows((S, S, S, S), ws_sc, ws_scales)
         S.dma_start(out=ws_w[:].bitcast(I32), in_=ws_words[0].bitcast(I32))
-        S.dma_start(out=sx_w[:].bitcast(I32), in_=sx_src)
         S.dma_start(out=tzt[:], in_=tz.rearrange("(h p) e -> p h e", p=P))
+        S.dma_start(out=sx_w[:].bitcast(I32), in_=sx_src)
         S.dma_start(o5[:], offs5)
         load_scale_rows((S, S, S, S), wb_sc, wb_scales)
         S.dma_start(out=wb_w[:].bitcast(I32), in_=wb_words[0].bitcast(I32))
@@ -91,7 +91,8 @@ def tile_list_tied_looked_skip_tabled_kernel(
         nc.vector.tensor_copy(out=ga_s[:], in_=xs[:].indirect(o1[:]))
         nc.vector.tensor_copy(out=gb_s[:], in_=xs[:].indirect(o2[:]))
         nc.vector.tensor_copy(out=ga_w[:], in_=xw[:].indirect(o1[:]))
-        nc.vector.tensor_copy(out=wsc_dealt[:], in_=wsc_raw[:].rearrange("p (q t) -> p t q", t=PACK))
+        nc.vector.tensor_copy(out=wsc_dealt[:, 0:1, :], in_=wsc_raw[:].rearrange("p (q t) -> p t q", t=PACK)[:, 0:1, :])
+        nc.vector.tensor_copy(out=wsc_dealt[:, 1:4, :], in_=wsc_raw[:].rearrange("p (q t) -> p t q", t=PACK)[:, 1:4, :])
         gb_w = sb.tile([P, J], U32, name="gb_w", tag="wsc_then_b", align_bytes=64)
         nc.vector.tensor_copy(out=gb_w[:], in_=xw[:].indirect(o2[:]))
 
@@ -114,7 +115,7 @@ def tile_list_tied_looked_skip_tabled_kernel(
             tile = sb.tile([P, J], F32, name="whole_%s%d" % (side, t), align_bytes=64)
             whole[side, t] = tile
             if eng == "S":
-                nc.scalar.activation(out=tile[:], in_=banks[side, t][:], func=ACT.Copy)
+                nc.scalar.copy(out=tile[:], in_=banks[side, t][:])
             else:
                 nc.vector.tensor_copy(out=tile[:], in_=banks[side, t][:])
 
@@ -132,29 +133,31 @@ def tile_list_tied_looked_skip_tabled_kernel(
         mm("a", 0)
         mm("a", 1)
         mm("a", 2)
+        mm("a", 3)
         mm("b", 0)
         mm("b", 1)
-        mm("a", 3)
         mm("b", 2)
         mm("b", 3)
         cp("a", 0, "S")
-        cp("a", 1, "V")
-        ga(0, "S")
+        cp("a", 1, "S")
         cp("a", 2, "V")
+        cp("a", 3, "V")
+        ga(0, "S")
         ga(1, "S")
         cp("b", 0, "V")
-        ga(2, "S")
         cp("b", 1, "V")
-        cp("a", 3, "S")
+        ga(2, "S")
+        ga(3, "S")
         gs(0)
         cp("b", 2, "S")
-        gs(1)
         cp("b", 3, "S")
-        ga(3, "S")
-        gs(2)
+        gs(1)
         nc.scalar.activation(out=hid[:, :, 0:2].rearrange("p (c i) t -> p c t i", i=4), in_=diff[:, 0:2, :].rearrange("p t (c i) -> p c t i", i=4), func=ACT.Abs)
+        gs(2)
         gs(3)
-        nc.scalar.activation(out=hid[:, :, 2:4].rearrange("p (c i) t -> p c t i", i=4), in_=diff[:, 2:4, :].rearrange("p t (c i) -> p c t i", i=4), func=ACT.Abs)
+        nc.scalar.activation(out=hid[:, 0:64, 2:4].rearrange("p (c i) t -> p c t i", i=4), in_=diff[:, 2:4, 0:64].rearrange("p t (c i) -> p c t i", i=4), func=ACT.Abs)
+        half = diff[:, 2:4, 64:128].rearrange("p t o -> p o t")
+        nc.vector.scalar_tensor_tensor(out=hid[:, 64:128, 2:4], in0=half, scalar=-1.0, in1=half, op0=ALU.mult, op1=ALU.max)
 
         acc = [psum.tile([P, O], F32, name="acc%d" % h, tag="bank_%s3" % "ab"[h]) for h in range(2)]
         for h in range(2):

from contextlib import ExitStack

import concourse.mybir as mybir

FLOPS = 335544320

F32 = mybir.dt.float32
BF16 = mybir.dt.bfloat16
I32 = mybir.dt.int32
U32 = mybir.dt.uint32
U16 = mybir.dt.uint16
U8 = mybir.dt.uint8
E4M3X4 = mybir.dt.float8_e4m3fn_x4
E5M2X4 = mybir.dt.float8_e5m2_x4
E2M1X4 = mybir.dt.float4_e2m1fn_x4
ACT = mybir.ActivationFunctionType
ALU = mybir.AluOpType

P = 128
PACK = 4
T, J, R, O, N, E = 2048, 256, 512, 128, 256, 1024


def load_scale_rows(queues, plane, scales):
    rows = scales[0].rearrange("(q r) c -> r q c", r=PACK)
    for r in range(PACK):
        queues[r].dma_start(out=plane[r:P:32, :].bitcast(I32), in_=rows[r].bitcast(I32))


def tile_list_tied_looked_skip_tabled_kernel(
    tc, xt_words, xt_scales, w_words, w_scales, wb_words, wb_scales, sx_words, sx_scales,
    ws_words, ws_scales, tz, offs, offs2, offs3, offs4, offs5, out,
):
    nc = tc.nc
    with ExitStack() as ctx:
        lists = ctx.enter_context(tc.tile_pool(name="lists", bufs=1))
        sb = ctx.enter_context(tc.tile_pool(name="sb", bufs=1))
        psum = ctx.enter_context(tc.psum_pool(name="psum", bufs=1))

        o1 = lists.tile([P, J // 16], U16, name="o1")
        o2 = lists.tile([P, J // 16], U16, name="o2")
        o3 = lists.tile([P, O // 16], U16, name="o3")
        o4 = lists.tile([P, O // 16], U16, name="o4")
        o5 = lists.tile([P, O // 16], U16, name="o5")

        xw = sb.tile([P, T], U32, name="xw", align_bytes=64)
        xs = sb.tile([P, T], U8, name="xs", align_bytes=64)
        w_raw = sb.tile([P, R], U16, name="w_raw", align_bytes=64)
        wsc_raw = sb.tile([P, R], U8, name="wsc_raw", tag="wsc_then_b", align_bytes=64)
        w_dealt = sb.tile([P, PACK, P], U16, name="w_dealt", align_bytes=64)
        wsc_dealt = sb.tile([P, PACK, P], U8, name="wsc_dealt", align_bytes=64)
        late = sb.tile([P, 2 * N + O], U8, name="late", align_bytes=64)
        wb_sc = late[:, 0:N]
        ws_sc = late[:, N : 2 * N]
        sx_sc = late[:, 2 * N : 2 * N + O]
        wb_w = sb.tile([P, 2 * N], U8, name="wb_w", align_bytes=64)
        ws_w = sb.tile([P, 2 * N], U8, name="ws_w", align_bytes=64)
        sx_w = sb.tile([P, O], U32, name="sx_w", align_bytes=64)
        tzt = sb.tile([P, 2, E], F32, name="tzt", align_bytes=64)

        nc.vector.memset(xs[:, 0 : T // 2].bitcast(I32), 0)
        nc.gpsimd.memset(xs[:, T // 2 : T].bitcast(I32), 0)
        nc.vector.memset(wsc_raw[:].bitcast(I32), 0)
        nc.vector.memset(late[:].bitcast(I32), 0)

        xw_src = xt_words[0].rearrange("p c t -> p (c t)").bitcast(I32)
        sx_src = sx_words[0].rearrange("p c t -> p (c t)").bitcast(I32)
        S, A, G = nc.sync, nc.scalar, nc.gpsimd
        S.dma_start(o1[:], offs)
        S.dma_start(o2[:], offs2)
        S.dma_start(out=w_raw[:].bitcast(I32), in_=w_words[0].bitcast(I32))
        load_scale_rows((S, A, S, A), xs, xt_scales)
        S.dma_start(out=xw[:, 0:2048].bitcast(I32), in_=xw_src[:, 0:2048])
        load_scale_rows((S, S, S, G), wsc_raw, w_scales)
        S.dma_start(o3[:], offs3)
        S.dma_start(o4[:], offs4)
        load_scale_rows((G, G, S, S), sx_sc, sx_scales)
        load_scale_rows((S, S, S, S), ws_sc, ws_scales)
        S.dma_start(out=ws_w[:].bitcast(I32), in_=ws_words[0].bitcast(I32))
        S.dma_start(out=tzt[:], in_=tz.rearrange("(h p) e -> p h e", p=P))
        S.dma_start(out=sx_w[:].bitcast(I32), in_=sx_src)
        S.dma_start(o5[:], offs5)
        load_scale_rows((S, S, S, S), wb_sc, wb_scales)
        S.dma_start(out=wb_w[:].bitcast(I32), in_=wb_words[0].bitcast(I32))

        ga_w = sb.tile([P, J], U32, name="ga_w", align_bytes=64)
        ga_s = sb.tile([P, J], U8, name="ga_s", align_bytes=64)
        gb_s = sb.tile([P, J], U8, name="gb_s", align_bytes=64)

        nc.scalar.copy(out=w_dealt[:], in_=w_raw[:].rearrange("p (q t) -> p t q", t=PACK))
        nc.vector.tensor_copy(out=ga_s[:], in_=xs[:].indirect(o1[:]))
        nc.vector.tensor_copy(out=gb_s[:], in_=xs[:].indirect(o2[:]))
        nc.vector.tensor_copy(out=ga_w[:], in_=xw[:].indirect(o1[:]))
        nc.vector.tensor_copy(out=wsc_dealt[:, 0:1, :], in_=wsc_raw[:].rearrange("p (q t) -> p t q", t=PACK)[:, 0:1, :])
        nc.vector.tensor_copy(out=wsc_dealt[:, 1:4, :], in_=wsc_raw[:].rearrange("p (q t) -> p t q", t=PACK)[:, 1:4, :])
        gb_w = sb.tile([P, J], U32, name="gb_w", tag="wsc_then_b", align_bytes=64)
        nc.vector.tensor_copy(out=gb_w[:], in_=xw[:].indirect(o2[:]))

        hid = sb.tile([P, O, PACK], BF16, name="hid", align_bytes=64)
        banks = {}
        whole = {}
        picked = sb.tile([P, PACK, O], F32, name="picked", tag="picked", align_bytes=64)
        diff = sb.tile([P, PACK, O], F32, name="diff", tag="diff", align_bytes=64)

        def mm(side, t):
            words, scales = (ga_w, ga_s) if side == "a" else (gb_w, gb_s)
            bank = psum.tile([P, J], F32, name="bank_%s%d" % (side, t), tag="bank_%s%d" % (side, t))
            banks[side, t] = bank
            nc.tensor.matmul_mx(
                out=bank[:], lhsT=w_dealt[:, t, :].bitcast(E2M1X4), lhsT_scale=wsc_dealt[:, t, :],
                rhs=words[:].bitcast(E5M2X4), rhs_scale=scales[:], start=True, stop=True,
            )

        def cp(side, t, eng):
            tile = sb.tile([P, J], F32, name="whole_%s%d" % (side, t), align_bytes=64)
            whole[side, t] = tile
            if eng == "S":
                nc.scalar.copy(out=tile[:], in_=banks[side, t][:])
            else:
                nc.vector.tensor_copy(out=tile[:], in_=banks[side, t][:])

        def ga(t, eng):
            if eng == "S":
                nc.scalar.activation(out=picked[:, t, :], in_=whole["a", t][:].indirect(o3[:]), func=ACT.Copy)
            else:
                nc.vector.tensor_copy(out=picked[:, t, :], in_=whole["a", t][:].indirect(o3[:]))

        def gs(t):
            nc.vector.tensor_tensor(
                out=diff[:, t, :], in0=whole["b", t][:].indirect(o4[:]), in1=picked[:, t, :], op=ALU.subtract
            )

        mm("a", 0)
        mm("a", 1)
        mm("a", 2)
        mm("a", 3)
        mm("b", 0)
        mm("b", 1)
        mm("b", 2)
        mm("b", 3)
        cp("a", 0, "S")
        cp("a", 1, "S")
        cp("a", 2, "V")
        cp("a", 3, "V")
        ga(0, "S")
        ga(1, "S")
        cp("b", 0, "V")
        cp("b", 1, "V")
        ga(2, "S")
        ga(3, "S")
        gs(0)
        cp("b", 2, "S")
        cp("b", 3, "S")
        gs(1)
        nc.scalar.activation(out=hid[:, :, 0:2].rearrange("p (c i) t -> p c t i", i=4), in_=diff[:, 0:2, :].rearrange("p t (c i) -> p c t i", i=4), func=ACT.Abs)
        gs(2)
        gs(3)
        nc.scalar.activation(out=hid[:, 0:64, 2:4].rearrange("p (c i) t -> p c t i", i=4), in_=diff[:, 2:4, 0:64].rearrange("p t (c i) -> p c t i", i=4), func=ACT.Abs)
        half = diff[:, 2:4, 64:128].rearrange("p t o -> p o t")
        nc.vector.scalar_tensor_tensor(out=hid[:, 64:128, 2:4], in0=half, scalar=-1.0, in1=half, op0=ALU.mult, op1=ALU.max)

        acc = [psum.tile([P, O], F32, name="acc%d" % h, tag="bank_%s3" % "ab"[h]) for h in range(2)]
        for h in range(2):
            nc.tensor.matmul_mx(
                out=acc[h][:], lhsT=ws_w[:, 2 * P * h : 2 * P * (h + 1)].bitcast(E2M1X4),
                lhsT_scale=ws_sc[:, P * h : P * (h + 1)],
                rhs=sx_w[:].bitcast(E4M3X4), rhs_scale=sx_sc, start=True, stop=False,
            )


        hq = sb.tile([P, O], U32, name="hq", align_bytes=64)
        hs = sb.tile([P, O], U8, name="hs", align_bytes=64)
        nc.vector.quantize_mx(out=hq[:].bitcast(E4M3X4), scales=hs[:], in_=hid[:].rearrange("p o t -> p (o t)"))

        tzg = sb.tile([P, 2, O], F32, name="tzg", tag="picked", align_bytes=64)
        for h in range(2):
            nc.scalar.activation(out=tzg[:, h, :], in_=tzt[:, h, :].indirect(o5[:]), func=ACT.Copy)

        for h in range(2):
            nc.tensor.matmul_mx(
                out=acc[h][:], lhsT=wb_w[:, 2 * P * h : 2 * P * (h + 1)].bitcast(E2M1X4),
                lhsT_scale=wb_sc[:, P * h : P * (h + 1)],
                rhs=hq[:].bitcast(E4M3X4), rhs_scale=hs[:], start=False, stop=True,
            )
        for h in range(2):
            res = sb.tile([P, O], F32, name="res%d" % h, align_bytes=64)
            nc.vector.tensor_tensor(out=res[:], in0=acc[h][:], in1=tzg[:, h, :], op=ALU.add)
            (S, A)[h].dma_start(out=out[P * h : P * (h + 1), :], in_=res[:])
